import numpy as np
import ml_dtypes


def mxq(x, axis, fmt="e4m3"):
    dtype, down = {"e4m3": (ml_dtypes.float8_e4m3fn, 7), "e5m2": (ml_dtypes.float8_e5m2, 14)}[fmt]
    v = np.moveaxis(np.asarray(x, np.float32).astype(ml_dtypes.bfloat16).astype(np.float64), axis, -1)
    blocks = v.reshape(v.shape[:-1] + (-1, 32))
    amax = np.abs(blocks).max(-1, keepdims=True)
    byte = np.maximum(np.where(amax > 0, np.frexp(amax)[1] - 1 + 127, 0) - down, 1)
    scale = np.exp2(byte - 127.0)
    codes = (blocks / scale).astype(np.float32).astype(dtype).astype(np.float64)
    return np.moveaxis((codes * scale).reshape(v.shape), -1, axis)


WIDE = False


def mx_kscale(k):
    if not WIDE:
        return np.ones(k)
    levels = np.array([10, -10, 5, -5, 0])
    if k % 512:
        return np.exp2(np.random.permutation(np.resize(levels, k // 32))).repeat(32)
    a = np.empty((k // 512, 16))
    for p in range(k // 512):
        a[p, :8] = np.random.permutation(np.resize(levels, 8))
        for g in range(8):
            far = levels[np.abs(levels - a[p, g]) >= 10]
            a[p, g + 8] = far[np.random.randint(len(far))]
    return np.exp2(a.ravel()).repeat(32)


def f64(x):
    return np.asarray(x).astype(np.float64)


def striped(idx):
    return np.tile(idx.reshape(-1, 16).T, (8, 1)).astype(np.uint16)


def unstriped(offs):
    return offs[:16].T.reshape(-1).astype(np.int64)


def striped8(idx):
    return np.concatenate([x.reshape(-1, 16).T for x in idx]).astype(np.uint16)


def runs(offs, k):
    lists = np.stack([offs[16 * r : 16 * r + 16].T.reshape(-1) for r in range(8)]).astype(np.int64)
    return lists[np.arange(k) % 512 // 64]


def pack_weight(w):
    k, n = w.shape
    w = f64(np.asarray(w, np.float32).astype(ml_dtypes.bfloat16)).reshape(k // 32, 32, n)
    amax = np.abs(w).max(1)
    byte = np.clip(np.where(amax > 0, np.frexp(amax)[1] - 1 + 127 - 7, 1), 1, 254)
    scaled = (w * np.exp2(127.0 - byte)[:, None, :]).reshape(k, n).astype(np.float32)
    words = np.ascontiguousarray(scaled.reshape(k // 512, 128, 4, n).transpose(0, 1, 3, 2)).astype(ml_dtypes.float8_e4m3fn).view(np.uint8)
    return words, np.ascontiguousarray(byte.astype(np.uint8).reshape(k // 512, 16, n))


def unpack_weight(words, scales):
    g, p, n, _ = words.shape
    vals = np.ascontiguousarray(words).view(ml_dtypes.float8_e4m3fn).astype(np.float64) * np.repeat(np.exp2(scales.astype(np.float64) - 127.0), 8, axis=1)[..., None]
    return vals.transpose(0, 1, 3, 2).reshape(g * 512, n)


E2M1 = np.array([0.0, 0.5, 1.0, 1.5, 2.0, 3.0, 4.0, 6.0, -0.0, -0.5, -1.0, -1.5, -2.0, -3.0, -4.0, -6.0])


def pack_fp4(w):
    k, n = w.shape
    w = f64(np.asarray(w, np.float32).astype(ml_dtypes.bfloat16)).reshape(k // 32, 32, n)
    amax = np.abs(w).max(1)
    mant, ex = np.frexp(amax / 6.0)
    byte = np.clip(np.where(amax > 0, np.where(mant > 0.5, ex, ex - 1) + 127, 1), 1, 254)
    scaled = (w * np.exp2(127.0 - byte)[:, None, :]).reshape(k, n).astype(np.float32)
    c = np.ascontiguousarray(scaled.reshape(k // 512, 128, 4, n).transpose(0, 1, 3, 2)).astype(ml_dtypes.float4_e2m1fn).view(np.uint8) & 0xF
    words = (c[..., 0::2] | (c[..., 1::2] << 4)).reshape(k // 512, 128, 2 * n)
    return np.ascontiguousarray(words), np.ascontiguousarray(byte.astype(np.uint8).reshape(k // 512, 16, n))


def unpack_fp4(words, scales):
    g, _, n = scales.shape
    words = np.ascontiguousarray(words).reshape(g, 128, n, 2)
    nib = np.empty((g, 128, n, 4), np.uint8)
    nib[..., 0::2] = words & 0xF
    nib[..., 1::2] = words >> 4
    vals = E2M1[nib] * np.repeat(np.exp2(scales.astype(np.float64) - 127.0), 8, axis=1)[..., None]
    return vals.transpose(0, 1, 3, 2).reshape(g * 512, n)


def planes(y):
    n, m = y.shape
    v = y.astype(np.float32).astype(ml_dtypes.bfloat16).astype(np.float64).reshape(n // 32, 32, m)
    top = np.abs(v).max(1)
    byte = np.clip(np.where(top > 0, np.frexp(top)[1] - 1 + 127 - 7, 1), 1, 254)
    codes = (v * np.exp2(127.0 - byte)[:, None, :]).reshape(n, m).astype(np.float32).astype(ml_dtypes.float8_e4m3fn).view(np.uint8)
    words = codes.reshape(n // 512, 128, 4, m).transpose(0, 1, 3, 2)
    return np.ascontiguousarray(words), np.ascontiguousarray(byte.astype(np.uint8).reshape(n // 512, 16, m))


K, T, S, V, N, H = 512, 2048, 1024, 512, 512, 512


def setup_inputs():
    n = np.random.standard_normal
    s = mx_kscale(K)[:, None]
    u = mx_kscale(H)
    packed_xT = pack_weight(n((K, T)) * s)
    packed_w3 = pack_fp4(n((H, N)) / np.sqrt(H) / u[:, None])
    return {
        "x_words": packed_xT[0],
        "x_scales": packed_xT[1],
        "w1": (n((K, H)) / np.sqrt(K) / s * u).astype(np.float32),
        "w2": (n((H, H)) / np.sqrt(H) / u[:, None] * u).astype(np.float32),
        "res": (2 * n((N, S))).astype(np.float32),
        "w3_words": packed_w3[0],
        "w3_scales": packed_w3[1],
        "offs": striped(np.random.permutation(T)[:S]),
        "nb": striped8(np.stack([np.random.permutation(S) for _ in range(8)])),
        "c1": striped8(np.stack([np.random.permutation(S)[:V] for _ in range(8)])),
        "c2": striped8(np.stack([np.random.permutation(S)[:V] for _ in range(8)])),
        "up": striped8(np.random.randint(0, V, (8, S))),
    }


def reference(x_words, x_scales, w1, w2, res, w3_words, w3_scales, offs, nb, c1, c2, up):
    xq = unpack_weight(x_words, x_scales)[:, unstriped(offs)]
    y = mxq(f64(w1), 0, "e4m3").T @ xq
    rs = y - (y[np.arange(H)[:, None], runs(nb, H)])
    c = rs[np.arange(H)[:, None], runs(c1, H)] + rs[np.arange(H)[:, None], runs(c2, H)]
    h = mxq(f64(w2), 0, "e4m3").T @ mxq(c, 0, "e4m3")
    z2 = rs - (h[np.arange(H)[:, None], runs(up, H)])
    out_0 = f64(res) + (unpack_fp4(w3_words, w3_scales).T @ mxq(z2, 0, "e4m3"))
    return (out_0,) + planes(out_0)

@@ -1,0 +1,223 @@
+from contextlib import ExitStack
+
+import concourse.mybir as mybir
+
+K, T, S, V, N, H = 512, 2048, 1024, 512, 512, 512
+FLOPS = 2 * K * H * S + 2 * H * H * V + 2 * H * N * S
+
+F32 = mybir.dt.float32
+BF16 = mybir.dt.bfloat16
+I32 = mybir.dt.int32
+U32 = mybir.dt.uint32
+U16 = mybir.dt.uint16
+U8 = mybir.dt.uint8
+FP8X4 = mybir.dt.float8_e4m3fn_x4
+FP4X4 = mybir.dt.float4_e2m1fn_x4
+ADD = mybir.AluOpType.add
+SUB = mybir.AluOpType.subtract
+
+P = 128
+PACK = 4
+BANK = 512
+CHUNKS = (256, 256, 256, 128, 128)
+C_SPLIT = 352
+
+
+def interleave(copy, dst, src):
+    copy(out=dst.rearrange("p (c i t) -> p c t i", i=4, t=PACK), in_=src.rearrange("p t (c i) -> p c t i", i=4))
+
+
+def deal(copy, dst, src):
+    copy(out=dst.rearrange("p t (m j) -> p m j t", j=PACK), in_=src.rearrange("p j (m t) -> p m j t", t=PACK))
+
+
+def tile_picked_twogrid_none_po_kernel(tc, x_words, x_scales, w1, w2, res, w3_words, w3_scales, offs, nb, c1, c2, up, out_0, out_1, out_2):
+    nc = tc.nc
+    with ExitStack() as ctx:
+        keep = ctx.enter_context(tc.tile_pool(name="keep", bufs=1))
+        ring = ctx.enter_context(tc.tile_pool(name="ring", bufs=2))
+        psum = ctx.enter_context(tc.psum_pool(name="psum", bufs=8))
+
+        def held(shape, dtype, name):
+            return keep.tile(shape, dtype, name=name, align_bytes=64)
+
+        def load_list(src, name):
+            tile = keep.tile(list(src.shape), U16, name=name)
+            nc.sync.dma_start(tile[:], src)
+            return tile
+
+        def load_scales(src, name):
+            tile = held([P, src.shape[2]], U8, name)
+            nc.vector.memset(tile[:].bitcast(I32), 0)
+            for q in range(4):
+                nc.sync.dma_start(out=tile[32 * q : 32 * q + 4, :].bitcast(I32), in_=src[0, 4 * q : 4 * q + 4, :].bitcast(I32))
+            return tile
+
+        def entries(lst, start, count):
+            return lst[:, start // 16 : (start + count) // 16]
+
+        offs_sb = load_list(offs, "offs_sb")
+        xs_all = load_scales(x_scales, "xs_all")
+        xw_all = held([P, T], U32, "xw_all")
+        nc.sync.dma_start(out=xw_all[:].bitcast(I32), in_=x_words[0].rearrange("p n t -> p (n t)").bitcast(I32))
+        w1_rows = w1.rearrange("(p j) c -> p j c", j=PACK)
+        w1_raw = []
+        for a in range(2):
+            raw = held([P, PACK, H // 2], F32, f"w1_raw{a}")
+            nc.sync.dma_start(out=raw[:], in_=w1_rows[:, :, a * (H // 2) : (a + 1) * (H // 2)])
+            w1_raw.append(raw)
+        nb_sb = load_list(nb, "nb_sb")
+        c1_sb = load_list(c1, "c1_sb")
+        c2_sb = load_list(c2, "c2_sb")
+        w3w_raw = held([P, 2 * N], U8, "w3w_raw")
+        nc.sync.dma_start(out=w3w_raw[:].bitcast(I32), in_=w3_words[0].bitcast(I32))
+        w3s_raw = load_scales(w3_scales, "w3s_raw")
+        up_sb = load_list(up, "up_sb")
+        w2_raw = held([P, PACK, H], F32, "w2_raw")
+        nc.sync.dma_start(out=w2_raw[:], in_=w2.rearrange("(p j) c -> p j c", j=PACK))
+        res_sb = held([P, PACK, S], F32, "res_sb")
+        nc.sync.dma_start(out=res_sb[:], in_=res.rearrange("(p t) s -> p t s", t=PACK))
+
+        xs = held([P, S], U8, "xs")
+        nc.vector.tensor_copy(xs[:], xs_all[:].indirect(offs_sb[:]))
+        xw = held([P, S], U32, "xw")
+        nc.vector.tensor_copy(xw[:], xw_all[:].indirect(offs_sb[:]))
+
+        w1_words = held([P, H], U32, "w1_words")
+        w1_scales = held([P, H], U8, "w1_scales")
+        w1_bf = []
+        for a, copy in enumerate((nc.scalar.copy, nc.vector.tensor_copy)):
+            bf = held([P, PACK, H // 2], BF16, f"w1_bf{a}")
+            deal(copy, bf[:], w1_raw[a][:])
+            w1_bf.append(bf)
+        for t in range(PACK):
+            for a in range(2):
+                cols = slice(P * t + 64 * a, P * t + 64 * (a + 1))
+                nc.vector.quantize_mx(out=w1_words[:, cols].bitcast(FP8X4), scales=w1_scales[:, cols], in_=w1_bf[a][:, t, :])
+
+        w3w = held([P, 2 * N], U8, "w3w")
+        nc.vector.tensor_copy(out=w3w[:].rearrange("p (t m b) -> p m t b", t=PACK, b=2), in_=w3w_raw[:].rearrange("p (m t b) -> p m t b", t=PACK, b=2))
+
+        y_win, y_plain = [], []
+        for t in range(PACK):
+            win = held([P, S], F32, f"y_win{t}")
+            plain = held([P, S], F32, f"y_plain{t}")
+            banks = []
+            for h in range(S // BANK):
+                cols = slice(BANK * h, BANK * (h + 1))
+                bank = psum.tile([P, BANK], F32, name="bank")
+                nc.tensor.matmul_mx(out=bank[:], lhsT=w1_words[:, P * t : P * (t + 1)].bitcast(FP8X4), lhsT_scale=w1_scales[:, P * t : P * (t + 1)],
+                                    rhs=xw[:, cols].bitcast(FP8X4), rhs_scale=xs[:, cols], start=True, stop=True)
+                copy = nc.vector.tensor_copy if (t, h) == (0, 1) else nc.scalar.copy
+                copy(out=win[:, cols], in_=bank[:])
+                banks.append(bank)
+            for h in range(S // BANK):
+                cols = slice(BANK * h, BANK * (h + 1))
+                nc.scalar.copy(out=plain[:, cols], in_=banks[h][:])
+            y_win.append(win)
+            y_plain.append(plain)
+
+        w2_bf = held([P, PACK, H], BF16, "w2_bf")
+        deal(nc.scalar.copy, w2_bf[:], w2_raw[:])
+        w2_words = held([P, H], U32, "w2_words")
+        w2_scales = held([P, H], U8, "w2_scales")
+
+        nrs = [held([P, S], F32, f"nrs{t}") for t in range(PACK)]
+        first = [held([P, V], F32, f"first{t}") for t in range(PACK)]
+        ncs = held([P, PACK, V], F32, "ncs")
+
+        def smooth(t, h):
+            cols = slice(BANK * h, BANK * (h + 1))
+            nc.vector.tensor_tensor(nrs[t][:, cols], y_win[t][:].indirect(entries(nb_sb, BANK * h, BANK)), y_plain[t][:, cols], SUB)
+
+        def fetch_c1(t):
+            nc.vector.tensor_copy(first[t][:], nrs[t][:].indirect(c1_sb[:]))
+
+        def fetch_c2(t):
+            nc.vector.tensor_tensor(ncs[:, t, :], nrs[t][:].indirect(c2_sb[:]), first[t][:], ADD)
+
+        smooth(0, 0)
+        smooth(0, 1)
+        for t in range(1, PACK):
+            smooth(t, 0)
+            fetch_c1(t - 1)
+            smooth(t, 1)
+            fetch_c2(t - 1)
+        nc.vector.quantize_mx(out=w2_words[:, :256].bitcast(FP8X4), scales=w2_scales[:, :256], in_=w2_bf[:, 0:2, :].rearrange("p t c -> p (t c)"))
+        fetch_c1(PACK - 1)
+        nc.vector.quantize_mx(out=w2_words[:, 256:].bitcast(FP8X4), scales=w2_scales[:, 256:], in_=w2_bf[:, 2:4, :].rearrange("p t c -> p (t c)"))
+        fetch_c2(PACK - 1)
+
+        c_bf = held([P, PACK * V], BF16, "c_bf")
+        interleave(nc.vector.tensor_copy, c_bf[:, : PACK * C_SPLIT], ncs[:, :, :C_SPLIT])
+        interleave(nc.scalar.copy, c_bf[:, PACK * C_SPLIT :], ncs[:, :, C_SPLIT:])
+        c_words = held([P, V], U32, "c_words")
+        c_scales = held([P, V], U8, "c_scales")
+        nc.vector.quantize_mx(out=c_words[:].bitcast(FP8X4), scales=c_scales[:], in_=c_bf[:])
+
+        w3s = held([P, N], U8, "w3s")
+        nc.vector.tensor_copy(out=w3s[:].rearrange("p (t m) -> p m t", t=PACK), in_=w3s_raw[:].rearrange("p (m t) -> p m t", t=PACK))
+
+        nh = []
+        for t in range(PACK):
+            bank = psum.tile([P, BANK], F32, name="bank")
+            nc.tensor.matmul_mx(out=bank[:], lhsT=w2_words[:, P * t : P * (t + 1)].bitcast(FP8X4), lhsT_scale=w2_scales[:, P * t : P * (t + 1)],
+                                rhs=c_words[:].bitcast(FP8X4), rhs_scale=c_scales[:], start=True, stop=True)
+            win = held([P, V], F32, f"nh{t}")
+            nc.scalar.copy(out=win[:], in_=bank[:])
+            nh.append(win)
+
+        o_words = held([P, S], U32, "o_words")
+        o_scales = held([P, S], U8, "o_scales")
+        out_rows = out_0.rearrange("(p t) s -> p t s", t=PACK)
+        out_words = out_1[0].rearrange("p n t -> p (n t)").bitcast(I32)
+        starts = [sum(CHUNKS[:i]) for i in range(len(CHUNKS))]
+        last = len(CHUNKS) - 1
+        z_bf, banks_of, o_bf = {}, {}, {}
+
+        def correct(i):
+            n = CHUNKS[i]
+            z = ring.tile([P, PACK, n], F32, name="z", align_bytes=64)
+            for t in range(PACK):
+                nc.vector.tensor_tensor(z[:, t, :], nh[t][:].indirect(entries(up_sb, starts[i], n)), nrs[t][:, starts[i] : starts[i] + n], SUB)
+            z_bf[i] = ring.tile([P, PACK * n], BF16, name="z_bf", align_bytes=64)
+            interleave(nc.vector.tensor_copy if i == last else nc.scalar.copy, z_bf[i][:], z[:])
+
+        def project(i):
+            n = CHUNKS[i]
+            z_words = ring.tile([P, n], U32, name="z_words", align_bytes=64)
+            z_scales = ring.tile([P, n], U8, name="z_scales", align_bytes=64)
+            nc.vector.quantize_mx(out=z_words[:].bitcast(FP8X4), scales=z_scales[:], in_=z_bf[i][:])
+            per_bank = BANK // n
+            banks_of[i] = []
+            for t0 in range(0, PACK, per_bank):
+                bank = psum.tile([P, per_bank, n], F32, name="bank")
+                for t in range(t0, t0 + per_bank):
+                    nc.tensor.matmul_mx(out=bank[:, t - t0, :], lhsT=w3w[:, 2 * P * t : 2 * P * (t + 1)].bitcast(FP4X4), lhsT_scale=w3s[:, P * t : P * (t + 1)],
+                                        rhs=z_words[:].bitcast(FP8X4), rhs_scale=z_scales[:], start=True, stop=True)
+                banks_of[i].append((t0, bank))
+
+        def add_res(i):
+            n = CHUNKS[i]
+            cols = slice(starts[i], starts[i] + n)
+            per_bank = BANK // n
+            o = held([P, PACK, n], F32, f"o{i}")
+            for t0, bank in banks_of[i]:
+                nc.vector.tensor_tensor(o[:, t0 : t0 + per_bank, :], bank[:], res_sb[:, t0 : t0 + per_bank, cols], ADD)
+            nc.sync.dma_start(out=out_rows[:, :, cols], in_=o[:])
+            o_bf[i] = ring.tile([P, PACK * n], BF16, name="o_bf", align_bytes=64)
+            interleave(nc.vector.tensor_copy if i == last else nc.scalar.copy, o_bf[i][:], o[:])
+
+        def hand_on(i):
+            cols = slice(starts[i], starts[i] + CHUNKS[i])
+            nc.vector.quantize_mx(out=o_words[:, cols].bitcast(FP8X4), scales=o_scales[:, cols], in_=o_bf[i][:])
+            nc.sync.dma_start(out=out_words[:, cols], in_=o_words[:, cols].bitcast(I32))
+
+        stages = (correct, project, add_res, hand_on)
+        for step in range(len(CHUNKS) + len(stages) - 1):
+            for lag, stage in enumerate(stages):
+                if 0 <= step - lag < len(CHUNKS):
+                    stage(step - lag)
+        for q in range(4):
+            queue = nc.sync if q % 2 else nc.scalar
+            queue.dma_start(out=out_2[0, 4 * q : 4 * q + 4, :].bitcast(I32), in_=o_scales[32 * q : 32 * q + 4, :].bitcast(I32))

@@ -18,17 +18,35 @@ SUB = mybir.AluOpType.subtract
 
 P = 128
 PACK = 4
+RUN = 4
 BANK = 512
+BANKS = 8
+QUADRANTS = 4
+HALF_H = H // 2
+HALF_V = V // 2
 CHUNKS = (256, 256, 256, 128, 128)
-C_SPLIT = 352
+W1_ON_SCALAR = 128
+C_ON_VECTOR = 160
 
 
 def interleave(copy, dst, src):
-    copy(out=dst.rearrange("p (c i t) -> p c t i", i=4, t=PACK), in_=src.rearrange("p t (c i) -> p c t i", i=4))
+    copy(out=as_words(dst), in_=as_runs(src))
+
+
+def as_words(dst):
+    return dst.rearrange("p (c i t) -> p c t i", i=RUN, t=PACK)
+
+
+def as_runs(src):
+    return src.rearrange("p t (c i) -> p c t i", i=RUN)
 
 
 def deal(copy, dst, src):
     copy(out=dst.rearrange("p t (m j) -> p m j t", j=PACK), in_=src.rearrange("p j (m t) -> p m j t", t=PACK))
+
+
+def entries(list_tile, start, count):
+    return list_tile[:, start // 16 : (start + count) // 16]
 
 
 def tile_picked_twogrid_none_po_kernel(tc, x_words, x_scales, w1, w2, res, w3_words, w3_scales, offs, nb, c1, c2, up, out_0, out_1, out_2):
@@ -36,10 +54,10 @@ def tile_picked_twogrid_none_po_kernel(tc, x_words, x_scales, w1, w2, res, w3_wo
     with ExitStack() as ctx:
         keep = ctx.enter_context(tc.tile_pool(name="keep", bufs=1))
         ring = ctx.enter_context(tc.tile_pool(name="ring", bufs=2))
-        psum = ctx.enter_context(tc.psum_pool(name="psum", bufs=8))
+        psum = ctx.enter_context(tc.psum_pool(name="psum", bufs=BANKS))
 
-        def held(shape, dtype, name):
-            return keep.tile(shape, dtype, name=name, align_bytes=64)
+        def held(shape, dtype, name, tag=None):
+            return keep.tile(shape, dtype, name=name, tag=tag or name, align_bytes=64)
 
         def load_list(src, name):
             tile = keep.tile(list(src.shape), U16, name=name)
@@ -49,72 +67,75 @@ def tile_picked_twogrid_none_po_kernel(tc, x_words, x_scales, w1, w2, res, w3_wo
         def load_scales(src, name):
             tile = held([P, src.shape[2]], U8, name)
             nc.vector.memset(tile[:].bitcast(I32), 0)
-            for q in range(4):
+            for q in range(QUADRANTS):
                 nc.sync.dma_start(out=tile[32 * q : 32 * q + 4, :].bitcast(I32), in_=src[0, 4 * q : 4 * q + 4, :].bitcast(I32))
             return tile
 
-        def entries(lst, start, count):
-            return lst[:, start // 16 : (start + count) // 16]
+        def quantise(words, scales, values):
+            nc.vector.quantize_mx(out=words.bitcast(FP8X4), scales=scales, in_=values)
+
+        def product(out, weights, weight_scales, t, words, scales):
+            nc.tensor.matmul_mx(out=out, lhsT=weights, lhsT_scale=weight_scales[:, P * t : P * (t + 1)], rhs=words.bitcast(FP8X4), rhs_scale=scales, start=True, stop=True)
 
         offs_sb = load_list(offs, "offs_sb")
-        xs_all = load_scales(x_scales, "xs_all")
-        xw_all = held([P, T], U32, "xw_all")
-        nc.sync.dma_start(out=xw_all[:].bitcast(I32), in_=x_words[0].rearrange("p n t -> p (n t)").bitcast(I32))
+        nb_sb = load_list(nb, "nb_sb")
+        c1_sb = load_list(c1, "c1_sb")
+        x_scales_all = load_scales(x_scales, "x_scales_all")
+        x_words_all = held([P, T], U32, "x_words_all")
+        nc.sync.dma_start(out=x_words_all[:].bitcast(I32), in_=x_words[0].rearrange("p n t -> p (n t)").bitcast(I32))
         w1_rows = w1.rearrange("(p j) c -> p j c", j=PACK)
         w1_raw = []
         for a in range(2):
-            raw = held([P, PACK, H // 2], F32, f"w1_raw{a}")
-            nc.sync.dma_start(out=raw[:], in_=w1_rows[:, :, a * (H // 2) : (a + 1) * (H // 2)])
+            raw = held([P, PACK, HALF_H], F32, f"w1_raw{a}")
+            nc.sync.dma_start(out=raw[:], in_=w1_rows[:, :, a * HALF_H : (a + 1) * HALF_H])
             w1_raw.append(raw)
-        nb_sb = load_list(nb, "nb_sb")
-        c1_sb = load_list(c1, "c1_sb")
         c2_sb = load_list(c2, "c2_sb")
-        w3w_raw = held([P, 2 * N], U8, "w3w_raw")
-        nc.sync.dma_start(out=w3w_raw[:].bitcast(I32), in_=w3_words[0].bitcast(I32))
-        w3s_raw = load_scales(w3_scales, "w3s_raw")
+        w3_words_raw = held([P, 2 * N], U8, "w3_words_raw")
+        nc.sync.dma_start(out=w3_words_raw[:].bitcast(I32), in_=w3_words[0].bitcast(I32))
+        w3_scales_raw = load_scales(w3_scales, "w3_scales_raw")
         up_sb = load_list(up, "up_sb")
         w2_raw = held([P, PACK, H], F32, "w2_raw")
         nc.sync.dma_start(out=w2_raw[:], in_=w2.rearrange("(p j) c -> p j c", j=PACK))
         res_sb = held([P, PACK, S], F32, "res_sb")
         nc.sync.dma_start(out=res_sb[:], in_=res.rearrange("(p t) s -> p t s", t=PACK))
 
-        xs = held([P, S], U8, "xs")
-        nc.vector.tensor_copy(xs[:], xs_all[:].indirect(offs_sb[:]))
-        xw = held([P, S], U32, "xw")
-        nc.vector.tensor_copy(xw[:], xw_all[:].indirect(offs_sb[:]))
+        xq_scales = held([P, S], U8, "xq_scales")
+        nc.vector.tensor_copy(xq_scales[:], x_scales_all[:].indirect(offs_sb[:]))
+        xq_words = held([P, S], U32, "xq_words")
+        nc.vector.tensor_copy(xq_words[:], x_words_all[:].indirect(offs_sb[:]))
 
         w1_words = held([P, H], U32, "w1_words")
         w1_scales = held([P, H], U8, "w1_scales")
-        w1_bf = []
-        for a, copy in enumerate((nc.scalar.copy, nc.vector.tensor_copy)):
-            bf = held([P, PACK, H // 2], BF16, f"w1_bf{a}")
-            deal(copy, bf[:], w1_raw[a][:])
-            w1_bf.append(bf)
-        for t in range(PACK):
-            for a in range(2):
-                cols = slice(P * t + 64 * a, P * t + 64 * (a + 1))
-                nc.vector.quantize_mx(out=w1_words[:, cols].bitcast(FP8X4), scales=w1_scales[:, cols], in_=w1_bf[a][:, t, :])
+        w1_bf = held([P, PACK, H], BF16, "w1_bf", "w1_bf_then_w3_words")
+        deal(nc.scalar.copy, w1_bf[:, :, :HALF_H], w1_raw[0][:])
+        deal(nc.scalar.copy, w1_bf[:, :, HALF_H : HALF_H + W1_ON_SCALAR], w1_raw[1][:, :, :W1_ON_SCALAR])
+        deal(nc.vector.tensor_copy, w1_bf[:, :, HALF_H + W1_ON_SCALAR :], w1_raw[1][:, :, W1_ON_SCALAR:])
+        for t0, t1 in ((0, 1), (1, 2), (2, PACK)):
+            cols = slice(P * t0, P * t1)
+            quantise(w1_words[:, cols], w1_scales[:, cols], w1_bf[:, t0:t1, :].rearrange("p t c -> p (t c)"))
 
-        w3w = held([P, 2 * N], U8, "w3w")
-        nc.vector.tensor_copy(out=w3w[:].rearrange("p (t m b) -> p m t b", t=PACK, b=2), in_=w3w_raw[:].rearrange("p (m t b) -> p m t b", t=PACK, b=2))
+        w3_words_dealt = held([P, 2 * N], U8, "w3_words_dealt", "w1_bf_then_w3_words")
+        nc.vector.tensor_copy(
+            out=w3_words_dealt[:].rearrange("p (t m b) -> p m t b", t=PACK, b=2),
+            in_=w3_words_raw[:].rearrange("p (m t b) -> p m t b", t=PACK, b=2),
+        )
 
-        y_win, y_plain = [], []
+        y_window, y_plain = [], []
         for t in range(PACK):
-            win = held([P, S], F32, f"y_win{t}")
+            window = held([P, S], F32, f"y_window{t}")
             plain = held([P, S], F32, f"y_plain{t}")
             banks = []
             for h in range(S // BANK):
                 cols = slice(BANK * h, BANK * (h + 1))
                 bank = psum.tile([P, BANK], F32, name="bank")
-                nc.tensor.matmul_mx(out=bank[:], lhsT=w1_words[:, P * t : P * (t + 1)].bitcast(FP8X4), lhsT_scale=w1_scales[:, P * t : P * (t + 1)],
-                                    rhs=xw[:, cols].bitcast(FP8X4), rhs_scale=xs[:, cols], start=True, stop=True)
-                copy = nc.vector.tensor_copy if (t, h) == (0, 1) else nc.scalar.copy
-                copy(out=win[:, cols], in_=bank[:])
+                product(bank[:], w1_words[:, P * t : P * (t + 1)].bitcast(FP8X4), w1_scales, t, xq_words[:, cols], xq_scales[:, cols])
+                completes_first_window = t == 0 and h == S // BANK - 1
+                copy = nc.vector.tensor_copy if completes_first_window else nc.scalar.copy
+                copy(out=window[:, cols], in_=bank[:])
                 banks.append(bank)
             for h in range(S // BANK):
-                cols = slice(BANK * h, BANK * (h + 1))
-                nc.scalar.copy(out=plain[:, cols], in_=banks[h][:])
-            y_win.append(win)
+                nc.scalar.copy(out=plain[:, BANK * h : BANK * (h + 1)], in_=banks[h][:])
+            y_window.append(window)
             y_plain.append(plain)
 
         w2_bf = held([P, PACK, H], BF16, "w2_bf")
@@ -122,102 +143,116 @@ def tile_picked_twogrid_none_po_kernel(tc, x_words, x_scales, w1, w2, res, w3_wo
         w2_words = held([P, H], U32, "w2_words")
         w2_scales = held([P, H], U8, "w2_scales")
 
-        nrs = [held([P, S], F32, f"nrs{t}") for t in range(PACK)]
-        first = [held([P, V], F32, f"first{t}") for t in range(PACK)]
-        ncs = held([P, PACK, V], F32, "ncs")
+        neg_rs = [held([P, S], F32, f"neg_rs{t}") for t in range(PACK)]
+        at_c1 = [held([P, V], F32, f"at_c1_{t}") for t in range(PACK)]
+        neg_c = held([P, PACK, V], F32, "neg_c")
 
         def smooth(t, h):
             cols = slice(BANK * h, BANK * (h + 1))
-            nc.vector.tensor_tensor(nrs[t][:, cols], y_win[t][:].indirect(entries(nb_sb, BANK * h, BANK)), y_plain[t][:, cols], SUB)
+            nc.vector.tensor_tensor(neg_rs[t][:, cols], y_window[t][:].indirect(entries(nb_sb, BANK * h, BANK)), y_plain[t][:, cols], SUB)
 
-        def fetch_c1(t):
-            nc.vector.tensor_copy(first[t][:], nrs[t][:].indirect(c1_sb[:]))
+        def fetch_c1(t, v0, v1):
+            nc.vector.tensor_copy(at_c1[t][:, v0:v1], neg_rs[t][:].indirect(entries(c1_sb, v0, v1 - v0)))
 
-        def fetch_c2(t):
-            nc.vector.tensor_tensor(ncs[:, t, :], nrs[t][:].indirect(c2_sb[:]), first[t][:], ADD)
+        def add_c2(t, v0, v1):
+            nc.vector.tensor_tensor(neg_c[:, t, v0:v1], neg_rs[t][:].indirect(entries(c2_sb, v0, v1 - v0)), at_c1[t][:, v0:v1], ADD)
 
         smooth(0, 0)
         smooth(0, 1)
         for t in range(1, PACK):
             smooth(t, 0)
-            fetch_c1(t - 1)
+            fetch_c1(t - 1, 0, V)
             smooth(t, 1)
-            fetch_c2(t - 1)
-        nc.vector.quantize_mx(out=w2_words[:, :256].bitcast(FP8X4), scales=w2_scales[:, :256], in_=w2_bf[:, 0:2, :].rearrange("p t c -> p (t c)"))
-        fetch_c1(PACK - 1)
-        nc.vector.quantize_mx(out=w2_words[:, 256:].bitcast(FP8X4), scales=w2_scales[:, 256:], in_=w2_bf[:, 2:4, :].rearrange("p t c -> p (t c)"))
-        fetch_c2(PACK - 1)
+            add_c2(t - 1, 0, V)
 
-        c_bf = held([P, PACK * V], BF16, "c_bf")
-        interleave(nc.vector.tensor_copy, c_bf[:, : PACK * C_SPLIT], ncs[:, :, :C_SPLIT])
-        interleave(nc.scalar.copy, c_bf[:, PACK * C_SPLIT :], ncs[:, :, C_SPLIT:])
-        c_words = held([P, V], U32, "c_words")
-        c_scales = held([P, V], U8, "c_scales")
-        nc.vector.quantize_mx(out=c_words[:].bitcast(FP8X4), scales=c_scales[:], in_=c_bf[:])
+        c_bf, c_words, c_scales = [], [], []
+        for a in range(2):
+            cols = slice(HALF_H * a, HALF_H * (a + 1))
+            fetch_c1(PACK - 1, HALF_V * a, HALF_V * (a + 1))
+            quantise(w2_words[:, cols], w2_scales[:, cols], w2_bf[:, 2 * a : 2 * a + 2, :].rearrange("p t c -> p (t c)"))
+            add_c2(PACK - 1, HALF_V * a, HALF_V * (a + 1))
+            c_bf.append(held([P, PACK * HALF_V], BF16, f"c_bf{a}"))
+            c_words.append(held([P, HALF_V], U32, f"c_words{a}"))
+            c_scales.append(held([P, HALF_V], U8, f"c_scales{a}"))
+            if a == 0:
+                interleave(nc.scalar.copy, c_bf[0][:], neg_c[:, :, :HALF_V])
+        neg_h = [held([P, V], F32, f"neg_h{t}") for t in range(PACK)]
 
-        w3s = held([P, N], U8, "w3s")
-        nc.vector.tensor_copy(out=w3s[:].rearrange("p (t m) -> p m t", t=PACK), in_=w3s_raw[:].rearrange("p (m t) -> p m t", t=PACK))
+        def solve(a):
+            quantise(c_words[a][:], c_scales[a][:], c_bf[a][:])
+            for t in range(PACK):
+                bank = psum.tile([P, HALF_V], F32, name="bank")
+                product(bank[:], w2_words[:, P * t : P * (t + 1)].bitcast(FP8X4), w2_scales, t, c_words[a][:], c_scales[a][:])
+                nc.scalar.copy(out=neg_h[t][:, HALF_V * a : HALF_V * (a + 1)], in_=bank[:])
 
-        nh = []
-        for t in range(PACK):
-            bank = psum.tile([P, BANK], F32, name="bank")
-            nc.tensor.matmul_mx(out=bank[:], lhsT=w2_words[:, P * t : P * (t + 1)].bitcast(FP8X4), lhsT_scale=w2_scales[:, P * t : P * (t + 1)],
-                                rhs=c_words[:].bitcast(FP8X4), rhs_scale=c_scales[:], start=True, stop=True)
-            win = held([P, V], F32, f"nh{t}")
-            nc.scalar.copy(out=win[:], in_=bank[:])
-            nh.append(win)
+        solve(0)
+        interleave(nc.vector.tensor_copy, c_bf[1][:, : PACK * C_ON_VECTOR], neg_c[:, :, HALF_V : HALF_V + C_ON_VECTOR])
+        interleave(nc.scalar.copy, c_bf[1][:, PACK * C_ON_VECTOR :], neg_c[:, :, HALF_V + C_ON_VECTOR :])
+        solve(1)
 
-        o_words = held([P, S], U32, "o_words")
-        o_scales = held([P, S], U8, "o_scales")
-        out_rows = out_0.rearrange("(p t) s -> p t s", t=PACK)
-        out_words = out_1[0].rearrange("p n t -> p (n t)").bitcast(I32)
+        w3_scales_dealt = held([P, N], U8, "w3_scales_dealt", "c_bf1")
+        nc.vector.tensor_copy(
+            out=w3_scales_dealt[:].rearrange("p (t m) -> p m t", t=PACK),
+            in_=w3_scales_raw[:].rearrange("p (m t) -> p m t", t=PACK),
+        )
+
+        out_words = held([P, S], U32, "out_words")
+        out_scales = held([P, S], U8, "out_scales")
+        out_0_planes = out_0.rearrange("(p t) s -> p t s", t=PACK)
+        out_1_words = out_1[0].rearrange("p n t -> p (n t)").bitcast(I32)
         starts = [sum(CHUNKS[:i]) for i in range(len(CHUNKS))]
         last = len(CHUNKS) - 1
-        z_bf, banks_of, o_bf = {}, {}, {}
+        z_bf, banks_of, out_bf = {}, {}, {}
 
         def correct(i):
             n = CHUNKS[i]
             z = ring.tile([P, PACK, n], F32, name="z", align_bytes=64)
             for t in range(PACK):
-                nc.vector.tensor_tensor(z[:, t, :], nh[t][:].indirect(entries(up_sb, starts[i], n)), nrs[t][:, starts[i] : starts[i] + n], SUB)
+                nc.vector.tensor_tensor(z[:, t, :], neg_h[t][:].indirect(entries(up_sb, starts[i], n)), neg_rs[t][:, starts[i] : starts[i] + n], SUB)
             z_bf[i] = ring.tile([P, PACK * n], BF16, name="z_bf", align_bytes=64)
-            interleave(nc.vector.tensor_copy if i == last else nc.scalar.copy, z_bf[i][:], z[:])
+            interleave(nc.scalar.copy, z_bf[i][:], z[:])
 
         def project(i):
             n = CHUNKS[i]
             z_words = ring.tile([P, n], U32, name="z_words", align_bytes=64)
             z_scales = ring.tile([P, n], U8, name="z_scales", align_bytes=64)
-            nc.vector.quantize_mx(out=z_words[:].bitcast(FP8X4), scales=z_scales[:], in_=z_bf[i][:])
+            quantise(z_words[:], z_scales[:], z_bf[i][:])
             per_bank = BANK // n
             banks_of[i] = []
             for t0 in range(0, PACK, per_bank):
                 bank = psum.tile([P, per_bank, n], F32, name="bank")
                 for t in range(t0, t0 + per_bank):
-                    nc.tensor.matmul_mx(out=bank[:, t - t0, :], lhsT=w3w[:, 2 * P * t : 2 * P * (t + 1)].bitcast(FP4X4), lhsT_scale=w3s[:, P * t : P * (t + 1)],
-                                        rhs=z_words[:].bitcast(FP8X4), rhs_scale=z_scales[:], start=True, stop=True)
-                banks_of[i].append((t0, bank))
+                    product(bank[:, t - t0, :], w3_words_dealt[:, 2 * P * t : 2 * P * (t + 1)].bitcast(FP4X4), w3_scales_dealt, t, z_words[:], z_scales[:])
+                banks_of[i].append((slice(t0, t0 + per_bank), bank))
 
         def add_res(i):
             n = CHUNKS[i]
             cols = slice(starts[i], starts[i] + n)
-            per_bank = BANK // n
-            o = held([P, PACK, n], F32, f"o{i}")
-            for t0, bank in banks_of[i]:
-                nc.vector.tensor_tensor(o[:, t0 : t0 + per_bank, :], bank[:], res_sb[:, t0 : t0 + per_bank, cols], ADD)
-            nc.sync.dma_start(out=out_rows[:, :, cols], in_=o[:])
-            o_bf[i] = ring.tile([P, PACK * n], BF16, name="o_bf", align_bytes=64)
-            interleave(nc.vector.tensor_copy if i == last else nc.scalar.copy, o_bf[i][:], o[:])
+            total = held([P, PACK, n], F32, f"total{i}")
+            if i < last:
+                out_bf[i] = ring.tile([P, PACK * CHUNKS[0]], BF16, name="out_bf", align_bytes=64)
+            else:
+                out_bf[i] = out_bf[i - 1]
+                nc.vector.tensor_tensor(as_words(out_bf[i][:, PACK * n :]), as_runs(banks_of[i][0][1][:]), as_runs(res_sb[:, :, cols]), ADD)
+            for planes, bank in banks_of[i]:
+                nc.vector.tensor_tensor(total[:, planes, :], bank[:], res_sb[:, planes, cols], ADD)
+            nc.sync.dma_start(out=out_0_planes[:, :, cols], in_=total[:])
+            if i < last:
+                interleave(nc.scalar.copy, out_bf[i][:, : PACK * n], total[:])
 
         def hand_on(i):
-            cols = slice(starts[i], starts[i] + CHUNKS[i])
-            nc.vector.quantize_mx(out=o_words[:, cols].bitcast(FP8X4), scales=o_scales[:, cols], in_=o_bf[i][:])
-            nc.sync.dma_start(out=out_words[:, cols], in_=o_words[:, cols].bitcast(I32))
+            if i == last - 1:
+                return
+            cols = slice(starts[i], starts[i + 1]) if i < last else slice(starts[last - 1], S)
+            quantise(out_words[:, cols], out_scales[:, cols], out_bf[i][:])
+            nc.sync.dma_start(out=out_1_words[:, cols], in_=out_words[:, cols].bitcast(I32))
 
         stages = (correct, project, add_res, hand_on)
         for step in range(len(CHUNKS) + len(stages) - 1):
-            for lag, stage in enumerate(stages):
+            for lag in reversed(range(len(stages))):
                 if 0 <= step - lag < len(CHUNKS):
-                    stage(step - lag)
-        for q in range(4):
+                    stages[lag](step - lag)
+
+        for q in range(QUADRANTS):
             queue = nc.sync if q % 2 else nc.scalar
-            queue.dma_start(out=out_2[0, 4 * q : 4 * q + 4, :].bitcast(I32), in_=o_scales[32 * q : 32 * q + 4, :].bitcast(I32))
+            queue.dma_start(out=out_2[0, 4 * q : 4 * q + 4, :].bitcast(I32), in_=out_scales[32 * q : 32 * q + 4, :].bitcast(I32))

from contextlib import ExitStack

import concourse.mybir as mybir

K, T, S, V, N, H = 512, 2048, 1024, 512, 512, 512
FLOPS = 2 * K * H * S + 2 * H * H * V + 2 * H * N * S

F32 = mybir.dt.float32
BF16 = mybir.dt.bfloat16
I32 = mybir.dt.int32
U32 = mybir.dt.uint32
U16 = mybir.dt.uint16
U8 = mybir.dt.uint8
FP8X4 = mybir.dt.float8_e4m3fn_x4
FP4X4 = mybir.dt.float4_e2m1fn_x4
ADD = mybir.AluOpType.add
SUB = mybir.AluOpType.subtract

P = 128
PACK = 4
RUN = 4
BANK = 512
BANKS = 8
QUADRANTS = 4
HALF_H = H // 2
HALF_V = V // 2
CHUNKS = (256, 256, 256, 128, 128)
W1_ON_SCALAR = 128
C_ON_VECTOR = 160


def interleave(copy, dst, src):
    copy(out=as_words(dst), in_=as_runs(src))


def as_words(dst):
    return dst.rearrange("p (c i t) -> p c t i", i=RUN, t=PACK)


def as_runs(src):
    return src.rearrange("p t (c i) -> p c t i", i=RUN)


def deal(copy, dst, src):
    copy(out=dst.rearrange("p t (m j) -> p m j t", j=PACK), in_=src.rearrange("p j (m t) -> p m j t", t=PACK))


def entries(list_tile, start, count):
    return list_tile[:, start // 16 : (start + count) // 16]


def tile_picked_twogrid_none_po_kernel(tc, x_words, x_scales, w1, w2, res, w3_words, w3_scales, offs, nb, c1, c2, up, out_0, out_1, out_2):
    nc = tc.nc
    with ExitStack() as ctx:
        keep = ctx.enter_context(tc.tile_pool(name="keep", bufs=1))
        ring = ctx.enter_context(tc.tile_pool(name="ring", bufs=2))
        psum = ctx.enter_context(tc.psum_pool(name="psum", bufs=BANKS))

        def held(shape, dtype, name, tag=None):
            return keep.tile(shape, dtype, name=name, tag=tag or name, align_bytes=64)

        def load_list(src, name):
            tile = keep.tile(list(src.shape), U16, name=name)
            nc.sync.dma_start(tile[:], src)
            return tile

        def load_scales(src, name):
            tile = held([P, src.shape[2]], U8, name)
            nc.vector.memset(tile[:].bitcast(I32), 0)
            for q in range(QUADRANTS):
                nc.sync.dma_start(out=tile[32 * q : 32 * q + 4, :].bitcast(I32), in_=src[0, 4 * q : 4 * q + 4, :].bitcast(I32))
            return tile

        def quantise(words, scales, values):
            nc.vector.quantize_mx(out=words.bitcast(FP8X4), scales=scales, in_=values)

        def product(out, weights, weight_scales, t, words, scales):
            nc.tensor.matmul_mx(out=out, lhsT=weights, lhsT_scale=weight_scales[:, P * t : P * (t + 1)], rhs=words.bitcast(FP8X4), rhs_scale=scales, start=True, stop=True)

        offs_sb = load_list(offs, "offs_sb")
        nb_sb = load_list(nb, "nb_sb")
        c1_sb = load_list(c1, "c1_sb")
        x_scales_all = load_scales(x_scales, "x_scales_all")
        x_words_all = held([P, T], U32, "x_words_all")
        nc.sync.dma_start(out=x_words_all[:].bitcast(I32), in_=x_words[0].rearrange("p n t -> p (n t)").bitcast(I32))
        w1_rows = w1.rearrange("(p j) c -> p j c", j=PACK)
        w1_raw = []
        for a in range(2):
            raw = held([P, PACK, HALF_H], F32, f"w1_raw{a}")
            nc.sync.dma_start(out=raw[:], in_=w1_rows[:, :, a * HALF_H : (a + 1) * HALF_H])
            w1_raw.append(raw)
        c2_sb = load_list(c2, "c2_sb")
        w3_words_raw = held([P, 2 * N], U8, "w3_words_raw")
        nc.sync.dma_start(out=w3_words_raw[:].bitcast(I32), in_=w3_words[0].bitcast(I32))
        w3_scales_raw = load_scales(w3_scales, "w3_scales_raw")
        up_sb = load_list(up, "up_sb")
        w2_raw = held([P, PACK, H], F32, "w2_raw")
        nc.sync.dma_start(out=w2_raw[:], in_=w2.rearrange("(p j) c -> p j c", j=PACK))
        res_sb = held([P, PACK, S], F32, "res_sb")
        nc.sync.dma_start(out=res_sb[:], in_=res.rearrange("(p t) s -> p t s", t=PACK))

        xq_scales = held([P, S], U8, "xq_scales")
        nc.vector.tensor_copy(xq_scales[:], x_scales_all[:].indirect(offs_sb[:]))
        xq_words = held([P, S], U32, "xq_words")
        nc.vector.tensor_copy(xq_words[:], x_words_all[:].indirect(offs_sb[:]))

        w1_words = held([P, H], U32, "w1_words")
        w1_scales = held([P, H], U8, "w1_scales")
        w1_bf = held([P, PACK, H], BF16, "w1_bf", "w1_bf_then_w3_words")
        deal(nc.scalar.copy, w1_bf[:, :, :HALF_H], w1_raw[0][:])
        deal(nc.scalar.copy, w1_bf[:, :, HALF_H : HALF_H + W1_ON_SCALAR], w1_raw[1][:, :, :W1_ON_SCALAR])
        deal(nc.vector.tensor_copy, w1_bf[:, :, HALF_H + W1_ON_SCALAR :], w1_raw[1][:, :, W1_ON_SCALAR:])
        for t0, t1 in ((0, 1), (1, 2), (2, PACK)):
            cols = slice(P * t0, P * t1)
            quantise(w1_words[:, cols], w1_scales[:, cols], w1_bf[:, t0:t1, :].rearrange("p t c -> p (t c)"))

        w3_words_dealt = held([P, 2 * N], U8, "w3_words_dealt", "w1_bf_then_w3_words")
        nc.vector.tensor_copy(
            out=w3_words_dealt[:].rearrange("p (t m b) -> p m t b", t=PACK, b=2),
            in_=w3_words_raw[:].rearrange("p (m t b) -> p m t b", t=PACK, b=2),
        )

        y_window, y_plain = [], []
        for t in range(PACK):
            window = held([P, S], F32, f"y_window{t}")
            plain = held([P, S], F32, f"y_plain{t}")
            banks = []
            for h in range(S // BANK):
                cols = slice(BANK * h, BANK * (h + 1))
                bank = psum.tile([P, BANK], F32, name="bank")
                product(bank[:], w1_words[:, P * t : P * (t + 1)].bitcast(FP8X4), w1_scales, t, xq_words[:, cols], xq_scales[:, cols])
                completes_first_window = t == 0 and h == S // BANK - 1
                copy = nc.vector.tensor_copy if completes_first_window else nc.scalar.copy
                copy(out=window[:, cols], in_=bank[:])
                banks.append(bank)
            for h in range(S // BANK):
                nc.scalar.copy(out=plain[:, BANK * h : BANK * (h + 1)], in_=banks[h][:])
            y_window.append(window)
            y_plain.append(plain)

        w2_bf = held([P, PACK, H], BF16, "w2_bf")
        deal(nc.scalar.copy, w2_bf[:], w2_raw[:])
        w2_words = held([P, H], U32, "w2_words")
        w2_scales = held([P, H], U8, "w2_scales")

        neg_rs = [held([P, S], F32, f"neg_rs{t}") for t in range(PACK)]
        at_c1 = [held([P, V], F32, f"at_c1_{t}") for t in range(PACK)]
        neg_c = held([P, PACK, V], F32, "neg_c")

        def smooth(t, h):
            cols = slice(BANK * h, BANK * (h + 1))
            nc.vector.tensor_tensor(neg_rs[t][:, cols], y_window[t][:].indirect(entries(nb_sb, BANK * h, BANK)), y_plain[t][:, cols], SUB)

        def fetch_c1(t, v0, v1):
            nc.vector.tensor_copy(at_c1[t][:, v0:v1], neg_rs[t][:].indirect(entries(c1_sb, v0, v1 - v0)))

        def add_c2(t, v0, v1):
            nc.vector.tensor_tensor(neg_c[:, t, v0:v1], neg_rs[t][:].indirect(entries(c2_sb, v0, v1 - v0)), at_c1[t][:, v0:v1], ADD)

        smooth(0, 0)
        smooth(0, 1)
        for t in range(1, PACK):
            smooth(t, 0)
            fetch_c1(t - 1, 0, V)
            smooth(t, 1)
            add_c2(t - 1, 0, V)

        c_bf, c_words, c_scales = [], [], []
        for a in range(2):
            cols = slice(HALF_H * a, HALF_H * (a + 1))
            fetch_c1(PACK - 1, HALF_V * a, HALF_V * (a + 1))
            quantise(w2_words[:, cols], w2_scales[:, cols], w2_bf[:, 2 * a : 2 * a + 2, :].rearrange("p t c -> p (t c)"))
            add_c2(PACK - 1, HALF_V * a, HALF_V * (a + 1))
            c_bf.append(held([P, PACK * HALF_V], BF16, f"c_bf{a}"))
            c_words.append(held([P, HALF_V], U32, f"c_words{a}"))
            c_scales.append(held([P, HALF_V], U8, f"c_scales{a}"))
            if a == 0:
                interleave(nc.scalar.copy, c_bf[0][:], neg_c[:, :, :HALF_V])
        neg_h = [held([P, V], F32, f"neg_h{t}") for t in range(PACK)]

        def solve(a):
            quantise(c_words[a][:], c_scales[a][:], c_bf[a][:])
            for t in range(PACK):
                bank = psum.tile([P, HALF_V], F32, name="bank")
                product(bank[:], w2_words[:, P * t : P * (t + 1)].bitcast(FP8X4), w2_scales, t, c_words[a][:], c_scales[a][:])
                nc.scalar.copy(out=neg_h[t][:, HALF_V * a : HALF_V * (a + 1)], in_=bank[:])

        solve(0)
        interleave(nc.vector.tensor_copy, c_bf[1][:, : PACK * C_ON_VECTOR], neg_c[:, :, HALF_V : HALF_V + C_ON_VECTOR])
        interleave(nc.scalar.copy, c_bf[1][:, PACK * C_ON_VECTOR :], neg_c[:, :, HALF_V + C_ON_VECTOR :])
        solve(1)

        w3_scales_dealt = held([P, N], U8, "w3_scales_dealt", "c_bf1")
        nc.vector.tensor_copy(
            out=w3_scales_dealt[:].rearrange("p (t m) -> p m t", t=PACK),
            in_=w3_scales_raw[:].rearrange("p (m t) -> p m t", t=PACK),
        )

        out_words = held([P, S], U32, "out_words")
        out_scales = held([P, S], U8, "out_scales")
        out_0_planes = out_0.rearrange("(p t) s -> p t s", t=PACK)
        out_1_words = out_1[0].rearrange("p n t -> p (n t)").bitcast(I32)
        starts = [sum(CHUNKS[:i]) for i in range(len(CHUNKS))]
        last = len(CHUNKS) - 1
        z_bf, banks_of, out_bf = {}, {}, {}

        def correct(i):
            n = CHUNKS[i]
            z = ring.tile([P, PACK, n], F32, name="z", align_bytes=64)
            for t in range(PACK):
                nc.vector.tensor_tensor(z[:, t, :], neg_h[t][:].indirect(entries(up_sb, starts[i], n)), neg_rs[t][:, starts[i] : starts[i] + n], SUB)
            z_bf[i] = ring.tile([P, PACK * n], BF16, name="z_bf", align_bytes=64)
            interleave(nc.scalar.copy, z_bf[i][:], z[:])

        def project(i):
            n = CHUNKS[i]
            z_words = ring.tile([P, n], U32, name="z_words", align_bytes=64)
            z_scales = ring.tile([P, n], U8, name="z_scales", align_bytes=64)
            quantise(z_words[:], z_scales[:], z_bf[i][:])
            per_bank = BANK // n
            banks_of[i] = []
            for t0 in range(0, PACK, per_bank):
                bank = psum.tile([P, per_bank, n], F32, name="bank")
                for t in range(t0, t0 + per_bank):
                    product(bank[:, t - t0, :], w3_words_dealt[:, 2 * P * t : 2 * P * (t + 1)].bitcast(FP4X4), w3_scales_dealt, t, z_words[:], z_scales[:])
                banks_of[i].append((slice(t0, t0 + per_bank), bank))

        def add_res(i):
            n = CHUNKS[i]
            cols = slice(starts[i], starts[i] + n)
            total = held([P, PACK, n], F32, f"total{i}")
            if i < last:
                out_bf[i] = ring.tile([P, PACK * CHUNKS[0]], BF16, name="out_bf", align_bytes=64)
            else:
                out_bf[i] = out_bf[i - 1]
                nc.vector.tensor_tensor(as_words(out_bf[i][:, PACK * n :]), as_runs(banks_of[i][0][1][:]), as_runs(res_sb[:, :, cols]), ADD)
            for planes, bank in banks_of[i]:
                nc.vector.tensor_tensor(total[:, planes, :], bank[:], res_sb[:, planes, cols], ADD)
            nc.sync.dma_start(out=out_0_planes[:, :, cols], in_=total[:])
            if i < last:
                interleave(nc.scalar.copy, out_bf[i][:, : PACK * n], total[:])

        def hand_on(i):
            if i == last - 1:
                return
            cols = slice(starts[i], starts[i + 1]) if i < last else slice(starts[last - 1], S)
            quantise(out_words[:, cols], out_scales[:, cols], out_bf[i][:])
            nc.sync.dma_start(out=out_1_words[:, cols], in_=out_words[:, cols].bitcast(I32))

        stages = (correct, project, add_res, hand_on)
        for step in range(len(CHUNKS) + len(stages) - 1):
            for lag in reversed(range(len(stages))):
                if 0 <= step - lag < len(CHUNKS):
                    stages[lag](step - lag)

        for q in range(QUADRANTS):
            queue = nc.sync if q % 2 else nc.scalar
            queue.dma_start(out=out_2[0, 4 * q : 4 * q + 4, :].bitcast(I32), in_=out_scales[32 * q : 32 * q + 4, :].bitcast(I32))
